import numpy as np, ml_dtypes
CORES = [8,9,12,13,16,17,20,21]
N = 8
TK = 128
D = 128 * N
def setup_inputs(rng):
    return {"x": (rng.standard_normal((N, 128, TK), dtype=np.float32) + 2 * rng.standard_normal((N, 1, TK), dtype=np.float32)).astype(ml_dtypes.bfloat16)}
def reference(x):
    X = x.astype(np.float64).reshape(D, TK)
    m = X.sum(axis=0) / D
    Z = X - m
    c = Z.T @ Z / D
    return {"c": np.broadcast_to(c.astype(np.float32), (N, TK, TK)), "m": np.broadcast_to(m.astype(np.float32), (N, 1, TK))}

@@ -1,0 +1,144 @@
+from concourse.bass import DstId, RemoteDMATransfer
+from concourse.mybir import dt, AluOpType
+
+W = 136
+P = 129
+F = "float32"
+SCRATCH = {
+    "xs": ("sbuf", [128, 128], "bfloat16"),
+    "xl": ("sbuf", [128, 4 * W], "bfloat16"),
+    "scale": ("sbuf", [128, P], F),
+    "pay": ("sbuf", [128, P], F),
+    "po": ("sbuf", [128, P], F),
+    "px": ("sbuf", [128, P], F),
+    "iot": ("sbuf", [128, 132], F),
+    "cst": ("sbuf", [128, 128], F),
+    "one_row": ("sbuf", [128, 128], F),
+    "neg_row": ("sbuf", [128, 128], F),
+    "two_t": ("sbuf", [128, 128], F),
+    "zero_t": ("sbuf", [128, 128], F),
+    "s1": ("sbuf", [128, 128], F),
+    "mn": ("sbuf", [128, 128], F),
+    "ident": ("sbuf", [128, 128], F),
+    "a_sb": ("sbuf", [128, 128], F),
+    "c_sb": ("sbuf", [128, 128], F),
+    "m_sb": ("sbuf", [128, 128], F),
+    "pg": ("psum", [128, 512], F),
+    "pd": ("psum", [128, 512], F),
+    "pm": ("psum", [128, 512], F),
+    "pq": ("psum", [128, 512], F),
+}
+SEMAPHORES = ["ld", "ls", "xa0", "xa1", "xa2", "xa3", "fill", "hpe", "hev", "v", "pe1", "pe2", "pe3",
+              "arr_o", "arr_x", "mrdy", "crdy", "stc", "stm"]
+
+
+def _dst(topo, core):
+    rid, pid, _se = topo.addr(core)
+    return DstId(rid=rid, pnc=pid)
+
+
+def _helper(g, core, T, topo, own_rank, far_rank, d_rows):
+    S = T.sem
+    for r in range(4):
+        g.vector.memset(T.xl[:, r * W + 128:r * W + W], 1.0).then_inc(S.fill, 1)
+    g.vector.memset(T.scale[:, :], 1.0 / d_rows).then_inc(S.fill, 1)
+    g.tensor.wait_ge(S.fill, 5)
+    for r in range(4):
+        g.tensor.wait_ge(S["xa%d" % r], 16)
+        mm = g.tensor.matmul(T.pg[:, 0:P], T.xl[:, r * W:r * W + 128], T.xl[:, r * W:r * W + P], r == 0, r == 3)
+    mm.then_inc(S.hpe, 1)
+    g.vector.wait_ge(S.fill, 5)
+    g.vector.wait_ge(S.hpe, 1)
+    g.vector.tensor_tensor(T.pay[:, :], T.pg[:, 0:P], T.scale[:, :], AluOpType.mult).then_inc(S.hev, 1)
+    g.wait_ge(S.hev, 1)
+    g.remote_dma_fused([
+        RemoteDMATransfer(dst_ids=[_dst(topo, far_rank)], dma_engine_mask=0x00FF, remote_sem=S.arr_x,
+                          src=T.pay[:, :], dst=T.px[:, :]),
+        RemoteDMATransfer(dst_ids=[_dst(topo, own_rank)], dma_engine_mask=0xFF00, remote_sem=S.arr_o,
+                          src=T.pay[:, :], dst=T.po[:, :]),
+    ], local_sem=S.ls)
+    g.wait_ge(S.ls, 16)
+
+
+def _rank(g, core, T, topo, slot, helpers):
+    S = T.sem
+    V, PE = g.vector, g.tensor
+    g.sync.dma_start(T.xs[:, :], T.x[:, :]).then_inc(S.ld, 16)
+    g.wait_ge(S.ld, 16)
+    g.remote_dma_fused([
+        RemoteDMATransfer(dst_ids=[_dst(topo, h) for h in helpers], dma_engine_mask=0xFFFF,
+                          remote_sem=S["xa%d" % slot], srcs=[T.xs[:, :]],
+                          dsts=[T.xl[:, slot * W:slot * W + 128] for _h in helpers]),
+    ], local_sem=S.ls)
+
+    n = [0]
+
+    def vi(ins):
+        ins.then_inc(S.v, 1)
+        n[0] += 1
+
+    vi(V.memset(T.iot[0:1, 0:1], 0.0))
+    vi(V.memset(T.iot[0:1, 128:129], 128.0))
+    for k in range(7):
+        vi(V.memset(T.cst[0:1, 2 ** k:2 ** (k + 1)], float(2 ** k)))
+    vi(V.memset(T.one_row[0:1, :], 1.0))
+    vi(V.memset(T.neg_row[0:1, :], -1.0))
+    vi(V.memset(T.two_t[:, :], 2.0))
+    vi(V.memset(T.zero_t[:, :], 0.0))
+    for k in range(7):
+        a = 2 ** k
+        V.wait_ge(S.v, n[0])
+        vi(V.tensor_tensor(T.iot[0:1, a:2 * a], T.iot[0:1, 0:a], T.cst[0:1, a:2 * a], AluOpType.add))
+    PE.wait_ge(S.v, n[0])
+    PE.matmul(T.pd[:, 0:128], T.iot[0:1, 1:129], T.one_row[0:1, :], True, False)
+    PE.matmul(T.pd[:, 0:128], T.neg_row[0:1, :], T.iot[0:1, 0:128], False, True).then_inc(S.pe1, 1)
+    V.wait_ge(S.v, n[0])
+    V.wait_ge(S.pe1, 1)
+    vi(V.tensor_tensor(T.s1[:, :], T.two_t[:, :], T.pd[:, 0:128], AluOpType.subtract))
+    V.wait_ge(S.v, n[0])
+    vi(V.tensor_tensor(T.mn[:, :], T.s1[:, :], T.pd[:, 0:128], AluOpType.min))
+    V.wait_ge(S.v, n[0])
+    vi(V.tensor_tensor(T.ident[:, :], T.mn[:, :], T.zero_t[:, :], AluOpType.max))
+    n_id = n[0]
+
+    PE.wait_ge(S.v, n_id)
+    PE.wait_ge(S.arr_o, 8)
+    PE.matmul(T.pm[0:1, 0:128], T.po[:, 128:129], T.ident[:, :], True, False)
+    PE.wait_ge(S.arr_x, 8)
+    PE.matmul(T.pm[0:1, 0:128], T.px[:, 128:129], T.ident[:, :], False, True).then_inc(S.pe2, 1)
+    V.wait_ge(S.v, n_id)
+    V.wait_ge(S.arr_o, 8)
+    V.wait_ge(S.arr_x, 8)
+    vi(V.tensor_tensor(T.a_sb[:, :], T.po[:, 0:128], T.px[:, 0:128], AluOpType.add))
+    V.wait_ge(S.pe2, 1)
+    V.tensor_copy(T.m_sb[0:1, :], T.pm[0:1, 0:128]).then_inc(S.mrdy, 1)
+    PE.wait_ge(S.mrdy, 1)
+    PE.matmul(T.pq[:, 0:128], T.m_sb[0:1, :], T.m_sb[0:1, :], True, True).then_inc(S.pe3, 1)
+    g.scalar.wait_ge(S.mrdy, 1)
+    g.scalar.dma_start(T.m[:, :], T.m_sb[0:1, :]).then_inc(S.stm, 16)
+    V.wait_ge(S.v, n[0])
+    V.wait_ge(S.pe3, 1)
+    V.tensor_tensor(T.c_sb[:, :], T.a_sb[:, :], T.pq[:, 0:128], AluOpType.subtract).then_inc(S.crdy, 1)
+    g.sync.wait_ge(S.crdy, 1)
+    g.sync.dma_start(T.c[:, :], T.c_sb[:, :]).then_inc(S.stc, 16)
+    g.sync.wait_ge(S.stc, 16)
+    g.scalar.wait_ge(S.stm, 16)
+    g.wait_ge(S.ls, 16)
+
+
+def rank_program(g, core, T, topo):
+    cores = list(T.cores)
+    chips = sorted(set(topo.chip(c) for c in cores))
+    d_rows = 128 * len(cores)
+    rank = T.rank_of(core)
+    if rank is not None:
+        mine = [c for c in cores if topo.chip(c) == topo.chip(core)]
+        hs = [c + 2 for c in mine]
+        order = [hs[0], hs[2], hs[1], hs[3]]
+        _rank(g, core, T, topo, mine.index(core), order)
+        return
+    own = core - 2
+    if own in cores:
+        other = chips[1] if topo.chip(core) == chips[0] else chips[0]
+        far = other * 8 + own % 8
+        _helper(g, core, T, topo, own, far, d_rows)

@@ -2,34 +2,27 @@ from concourse.bass import DstId, RemoteDMATransfer
 from concourse.mybir import dt, AluOpType
 
 W = 136
-P = 129
+P = 130
 F = "float32"
 SCRATCH = {
-    "xs": ("sbuf", [128, 128], "bfloat16"),
+    "xs": ("sbuf", [128, W], "bfloat16"),
     "xl": ("sbuf", [128, 4 * W], "bfloat16"),
-    "scale": ("sbuf", [128, P], F),
+    "scale": ("sbuf", [128, 128], F),
     "pay": ("sbuf", [128, P], F),
     "po": ("sbuf", [128, P], F),
     "px": ("sbuf", [128, P], F),
-    "iot": ("sbuf", [128, 132], F),
-    "cst": ("sbuf", [128, 128], F),
-    "one_row": ("sbuf", [128, 128], F),
-    "neg_row": ("sbuf", [128, 128], F),
-    "two_t": ("sbuf", [128, 128], F),
-    "zero_t": ("sbuf", [128, 128], F),
-    "s1": ("sbuf", [128, 128], F),
-    "mn": ("sbuf", [128, 128], F),
-    "ident": ("sbuf", [128, 128], F),
+    "mext": ("sbuf", [128, 132], F),
+    "q2": ("sbuf", [128, 4], F),
+    "crn": ("sbuf", [128, 4], F),
     "a_sb": ("sbuf", [128, 128], F),
     "c_sb": ("sbuf", [128, 128], F),
-    "m_sb": ("sbuf", [128, 128], F),
     "pg": ("psum", [128, 512], F),
-    "pd": ("psum", [128, 512], F),
-    "pm": ("psum", [128, 512], F),
+    "pz": ("psum", [128, 512], F),
+    "ppo": ("psum", [128, 512], F),
     "pq": ("psum", [128, 512], F),
 }
-SEMAPHORES = ["ld", "ls", "xa0", "xa1", "xa2", "xa3", "fill", "hpe", "hev", "v", "pe1", "pe2", "pe3",
-              "arr_o", "arr_x", "mrdy", "crdy", "stc", "stm"]
+SEMAPHORES = ["ld", "ones", "ls", "xa0", "xa1", "xa2", "xa3", "fill", "hz", "hpe", "hev", "vq", "pe3",
+              "arr_o", "arr_x", "mrdy", "prdy", "crdy", "stc", "stm", "stp", "stk"]
 
 
 def _dst(topo, core):
@@ -37,20 +30,24 @@ def _dst(topo, core):
     return DstId(rid=rid, pnc=pid)
 
 
-def _helper(g, core, T, topo, own_rank, far_rank, d_rows):
+def _helper(g, core, T, topo, own_rank, far_rank, d_rows, blocks):
     S = T.sem
-    for r in range(4):
-        g.vector.memset(T.xl[:, r * W + 128:r * W + W], 1.0).then_inc(S.fill, 1)
-    g.vector.memset(T.scale[:, :], 1.0 / d_rows).then_inc(S.fill, 1)
-    g.tensor.wait_ge(S.fill, 5)
-    for r in range(4):
-        g.tensor.wait_ge(S["xa%d" % r], 16)
-        mm = g.tensor.matmul(T.pg[:, 0:P], T.xl[:, r * W:r * W + 128], T.xl[:, r * W:r * W + P], r == 0, r == 3)
+    V, PE = g.vector, g.tensor
+    V.memset(T.scale[:, :], 1.0 / d_rows).then_inc(S.fill, 1)
+    V.memset(T.pay[:, 128:P], 0.0).then_inc(S.fill, 1)
+    for i, r in enumerate(blocks):
+        b = r * W
+        PE.wait_ge(S["xa%d" % r], 16)
+        tz = PE.matmul(T.pz[0:1, 0:2], T.xl[:, b + 135:b + 136], T.xl[:, b + 134:b + 136], i == 0, i == 3)
+        mm = PE.matmul(T.pg[:, 0:128], T.xl[:, b + 7:b + 135], T.xl[:, b + 8:b + 136], i == 0, i == 3)
+    tz.then_inc(S.hz, 1)
     mm.then_inc(S.hpe, 1)
-    g.vector.wait_ge(S.fill, 5)
-    g.vector.wait_ge(S.hpe, 1)
-    g.vector.tensor_tensor(T.pay[:, :], T.pg[:, 0:P], T.scale[:, :], AluOpType.mult).then_inc(S.hev, 1)
-    g.wait_ge(S.hev, 1)
+    V.wait_ge(S.fill, 2)
+    V.wait_ge(S.hz, 1)
+    V.tensor_tensor(T.pay[0:1, 128:P], T.pz[0:1, 0:2], T.scale[0:1, 0:2], AluOpType.mult).then_inc(S.hev, 1)
+    V.wait_ge(S.hpe, 1)
+    V.tensor_tensor(T.pay[:, 0:128], T.pg[:, 0:128], T.scale[:, :], AluOpType.mult).then_inc(S.hev, 1)
+    g.wait_ge(S.hev, 2)
     g.remote_dma_fused([
         RemoteDMATransfer(dst_ids=[_dst(topo, far_rank)], dma_engine_mask=0x00FF, remote_sem=S.arr_x,
                           src=T.pay[:, :], dst=T.px[:, :]),
@@ -63,66 +60,48 @@ def _helper(g, core, T, topo, own_rank, far_rank, d_rows):
 def _rank(g, core, T, topo, slot, helpers):
     S = T.sem
     V, PE = g.vector, g.tensor
-    g.sync.dma_start(T.xs[:, :], T.x[:, :]).then_inc(S.ld, 16)
+    g.sync.dma_start(T.xs[:, 8:W], T.x[:, :]).then_inc(S.ld, 16)
+    V.memset(T.xs[:, 0:8], 1.0).then_inc(S.ones, 1)
+    V.memset(T.mext[0:1, 0:1], 0.0).then_inc(S.ones, 1)
+    g.wait_ge(S.ones, 2)
     g.wait_ge(S.ld, 16)
+    b = slot * W
     g.remote_dma_fused([
         RemoteDMATransfer(dst_ids=[_dst(topo, h) for h in helpers], dma_engine_mask=0xFFFF,
-                          remote_sem=S["xa%d" % slot], srcs=[T.xs[:, :]],
-                          dsts=[T.xl[:, slot * W:slot * W + 128] for _h in helpers]),
+                          remote_sem=S["xa%d" % slot], srcs=[T.xs[:, 7:W]],
+                          dsts=[T.xl[:, b + 7:b + W] for _h in helpers]),
     ], local_sem=S.ls)
 
-    n = [0]
-
-    def vi(ins):
-        ins.then_inc(S.v, 1)
-        n[0] += 1
-
-    vi(V.memset(T.iot[0:1, 0:1], 0.0))
-    vi(V.memset(T.iot[0:1, 128:129], 128.0))
-    for k in range(7):
-        vi(V.memset(T.cst[0:1, 2 ** k:2 ** (k + 1)], float(2 ** k)))
-    vi(V.memset(T.one_row[0:1, :], 1.0))
-    vi(V.memset(T.neg_row[0:1, :], -1.0))
-    vi(V.memset(T.two_t[:, :], 2.0))
-    vi(V.memset(T.zero_t[:, :], 0.0))
-    for k in range(7):
-        a = 2 ** k
-        V.wait_ge(S.v, n[0])
-        vi(V.tensor_tensor(T.iot[0:1, a:2 * a], T.iot[0:1, 0:a], T.cst[0:1, a:2 * a], AluOpType.add))
-    PE.wait_ge(S.v, n[0])
-    PE.matmul(T.pd[:, 0:128], T.iot[0:1, 1:129], T.one_row[0:1, :], True, False)
-    PE.matmul(T.pd[:, 0:128], T.neg_row[0:1, :], T.iot[0:1, 0:128], False, True).then_inc(S.pe1, 1)
-    V.wait_ge(S.v, n[0])
-    V.wait_ge(S.pe1, 1)
-    vi(V.tensor_tensor(T.s1[:, :], T.two_t[:, :], T.pd[:, 0:128], AluOpType.subtract))
-    V.wait_ge(S.v, n[0])
-    vi(V.tensor_tensor(T.mn[:, :], T.s1[:, :], T.pd[:, 0:128], AluOpType.min))
-    V.wait_ge(S.v, n[0])
-    vi(V.tensor_tensor(T.ident[:, :], T.mn[:, :], T.zero_t[:, :], AluOpType.max))
-    n_id = n[0]
-
-    PE.wait_ge(S.v, n_id)
-    PE.wait_ge(S.arr_o, 8)
-    PE.matmul(T.pm[0:1, 0:128], T.po[:, 128:129], T.ident[:, :], True, False)
-    PE.wait_ge(S.arr_x, 8)
-    PE.matmul(T.pm[0:1, 0:128], T.px[:, 128:129], T.ident[:, :], False, True).then_inc(S.pe2, 1)
-    V.wait_ge(S.v, n_id)
+    V.wait_ge(S.ones, 2)
     V.wait_ge(S.arr_o, 8)
+    V.tensor_copy(T.ppo[:, 0:P], T.po[:, :]).then_inc(S.vq, 1)
+    V.wait_ge(S.vq, 1)
     V.wait_ge(S.arr_x, 8)
-    vi(V.tensor_tensor(T.a_sb[:, :], T.po[:, 0:128], T.px[:, 0:128], AluOpType.add))
-    V.wait_ge(S.pe2, 1)
-    V.tensor_copy(T.m_sb[0:1, :], T.pm[0:1, 0:128]).then_inc(S.mrdy, 1)
+    V.tensor_tensor(T.mext[0:1, 1:131], T.ppo[0:1, 0:P], T.px[0:1, :], AluOpType.add).then_inc(S.mrdy, 1)
+    PE.wait_ge(S.ones, 2)
     PE.wait_ge(S.mrdy, 1)
-    PE.matmul(T.pq[:, 0:128], T.m_sb[0:1, :], T.m_sb[0:1, :], True, True).then_inc(S.pe3, 1)
-    g.scalar.wait_ge(S.mrdy, 1)
-    g.scalar.dma_start(T.m[:, :], T.m_sb[0:1, :]).then_inc(S.stm, 16)
-    V.wait_ge(S.v, n[0])
+    PE.matmul(T.pq[:, 0:128], T.mext[0:1, 0:128], T.mext[0:1, 1:129], True, True).then_inc(S.pe3, 1)
+    V.tensor_tensor(T.a_sb[:, :], T.ppo[:, 0:128], T.px[:, 0:128], AluOpType.add).then_inc(S.vq, 1)
+    V.wait_ge(S.mrdy, 1)
+    V.tensor_tensor(T.q2[0:1, 0:1], T.mext[0:1, 127:128], T.mext[0:1, 128:129], AluOpType.mult).then_inc(S.vq, 1)
+    V.tensor_tensor(T.q2[0:1, 1:2], T.mext[0:1, 128:129], T.mext[0:1, 128:129], AluOpType.mult).then_inc(S.vq, 1)
+    V.wait_ge(S.vq, 4)
+    V.tensor_tensor(T.crn[0:1, 0:2], T.mext[0:1, 129:131], T.q2[0:1, 0:2], AluOpType.subtract).then_inc(S.prdy, 1)
     V.wait_ge(S.pe3, 1)
     V.tensor_tensor(T.c_sb[:, :], T.a_sb[:, :], T.pq[:, 0:128], AluOpType.subtract).then_inc(S.crdy, 1)
+
     g.sync.wait_ge(S.crdy, 1)
-    g.sync.dma_start(T.c[:, :], T.c_sb[:, :]).then_inc(S.stc, 16)
+    g.sync.dma_start(T.c[0:127, :], T.c_sb[1:128, :]).then_inc(S.stc, 16)
+    g.scalar.wait_ge(S.mrdy, 1)
+    g.scalar.dma_start(T.m[:, :], T.mext[0:1, 1:129]).then_inc(S.stm, 16)
+    g.scalar.wait_ge(S.prdy, 1)
+    g.scalar.dma_start(T.c[127:128, 126:128], T.crn[0:1, 0:2]).then_inc(S.stp, 16)
+    g.scalar.wait_ge(S.crdy, 1)
+    g.scalar.dma_start(T.c[127:128, 0:126], T.c_sb[1:127, 127:128]).then_inc(S.stk, 16)
     g.sync.wait_ge(S.stc, 16)
     g.scalar.wait_ge(S.stm, 16)
+    g.scalar.wait_ge(S.stp, 16)
+    g.scalar.wait_ge(S.stk, 16)
     g.wait_ge(S.ls, 16)
 
 
@@ -133,12 +112,14 @@ def rank_program(g, core, T, topo):
     rank = T.rank_of(core)
     if rank is not None:
         mine = [c for c in cores if topo.chip(c) == topo.chip(core)]
+        slot = mine.index(core)
         hs = [c + 2 for c in mine]
-        order = [hs[0], hs[2], hs[1], hs[3]]
-        _rank(g, core, T, topo, mine.index(core), order)
+        order = [hs[0], hs[2], hs[1], hs[3]] if slot < 2 else [hs[2], hs[0], hs[3], hs[1]]
+        _rank(g, core, T, topo, slot, order)
         return
     own = core - 2
     if own in cores:
         other = chips[1] if topo.chip(core) == chips[0] else chips[0]
         far = other * 8 + own % 8
-        _helper(g, core, T, topo, own, far, d_rows)
+        blocks = [0, 1, 2, 3] if own % 8 < 4 else [2, 3, 0, 1]
+        _helper(g, core, T, topo, own, far, d_rows, blocks)

from concourse.bass import DstId, RemoteDMATransfer
from concourse.mybir import dt, AluOpType

W = 136
P = 130
F = "float32"
SCRATCH = {
    "xs": ("sbuf", [128, W], "bfloat16"),
    "xl": ("sbuf", [128, 4 * W], "bfloat16"),
    "scale": ("sbuf", [128, 128], F),
    "pay": ("sbuf", [128, P], F),
    "po": ("sbuf", [128, P], F),
    "px": ("sbuf", [128, P], F),
    "mext": ("sbuf", [128, 132], F),
    "q2": ("sbuf", [128, 4], F),
    "crn": ("sbuf", [128, 4], F),
    "a_sb": ("sbuf", [128, 128], F),
    "c_sb": ("sbuf", [128, 128], F),
    "pg": ("psum", [128, 512], F),
    "pz": ("psum", [128, 512], F),
    "ppo": ("psum", [128, 512], F),
    "pq": ("psum", [128, 512], F),
}
SEMAPHORES = ["ld", "ones", "ls", "xa0", "xa1", "xa2", "xa3", "fill", "hz", "hpe", "hev", "vq", "pe3",
              "arr_o", "arr_x", "mrdy", "prdy", "crdy", "stc", "stm", "stp", "stk"]


def _dst(topo, core):
    rid, pid, _se = topo.addr(core)
    return DstId(rid=rid, pnc=pid)


def _helper(g, core, T, topo, own_rank, far_rank, d_rows, blocks):
    S = T.sem
    V, PE = g.vector, g.tensor
    V.memset(T.scale[:, :], 1.0 / d_rows).then_inc(S.fill, 1)
    V.memset(T.pay[:, 128:P], 0.0).then_inc(S.fill, 1)
    for i, r in enumerate(blocks):
        b = r * W
        PE.wait_ge(S["xa%d" % r], 16)
        tz = PE.matmul(T.pz[0:1, 0:2], T.xl[:, b + 135:b + 136], T.xl[:, b + 134:b + 136], i == 0, i == 3)
        mm = PE.matmul(T.pg[:, 0:128], T.xl[:, b + 7:b + 135], T.xl[:, b + 8:b + 136], i == 0, i == 3)
    tz.then_inc(S.hz, 1)
    mm.then_inc(S.hpe, 1)
    V.wait_ge(S.fill, 2)
    V.wait_ge(S.hz, 1)
    V.tensor_tensor(T.pay[0:1, 128:P], T.pz[0:1, 0:2], T.scale[0:1, 0:2], AluOpType.mult).then_inc(S.hev, 1)
    V.wait_ge(S.hpe, 1)
    V.tensor_tensor(T.pay[:, 0:128], T.pg[:, 0:128], T.scale[:, :], AluOpType.mult).then_inc(S.hev, 1)
    g.wait_ge(S.hev, 2)
    g.remote_dma_fused([
        RemoteDMATransfer(dst_ids=[_dst(topo, far_rank)], dma_engine_mask=0x00FF, remote_sem=S.arr_x,
                          src=T.pay[:, :], dst=T.px[:, :]),
        RemoteDMATransfer(dst_ids=[_dst(topo, own_rank)], dma_engine_mask=0xFF00, remote_sem=S.arr_o,
                          src=T.pay[:, :], dst=T.po[:, :]),
    ], local_sem=S.ls)
    g.wait_ge(S.ls, 16)


def _rank(g, core, T, topo, slot, helpers):
    S = T.sem
    V, PE = g.vector, g.tensor
    g.sync.dma_start(T.xs[:, 8:W], T.x[:, :]).then_inc(S.ld, 16)
    V.memset(T.xs[:, 0:8], 1.0).then_inc(S.ones, 1)
    V.memset(T.mext[0:1, 0:1], 0.0).then_inc(S.ones, 1)
    g.wait_ge(S.ones, 2)
    g.wait_ge(S.ld, 16)
    b = slot * W
    g.remote_dma_fused([
        RemoteDMATransfer(dst_ids=[_dst(topo, h) for h in helpers], dma_engine_mask=0xFFFF,
                          remote_sem=S["xa%d" % slot], srcs=[T.xs[:, 7:W]],
                          dsts=[T.xl[:, b + 7:b + W] for _h in helpers]),
    ], local_sem=S.ls)

    V.wait_ge(S.ones, 2)
    V.wait_ge(S.arr_o, 8)
    V.tensor_copy(T.ppo[:, 0:P], T.po[:, :]).then_inc(S.vq, 1)
    V.wait_ge(S.vq, 1)
    V.wait_ge(S.arr_x, 8)
    V.tensor_tensor(T.mext[0:1, 1:131], T.ppo[0:1, 0:P], T.px[0:1, :], AluOpType.add).then_inc(S.mrdy, 1)
    PE.wait_ge(S.ones, 2)
    PE.wait_ge(S.mrdy, 1)
    PE.matmul(T.pq[:, 0:128], T.mext[0:1, 0:128], T.mext[0:1, 1:129], True, True).then_inc(S.pe3, 1)
    V.tensor_tensor(T.a_sb[:, :], T.ppo[:, 0:128], T.px[:, 0:128], AluOpType.add).then_inc(S.vq, 1)
    V.wait_ge(S.mrdy, 1)
    V.tensor_tensor(T.q2[0:1, 0:1], T.mext[0:1, 127:128], T.mext[0:1, 128:129], AluOpType.mult).then_inc(S.vq, 1)
    V.tensor_tensor(T.q2[0:1, 1:2], T.mext[0:1, 128:129], T.mext[0:1, 128:129], AluOpType.mult).then_inc(S.vq, 1)
    V.wait_ge(S.vq, 4)
    V.tensor_tensor(T.crn[0:1, 0:2], T.mext[0:1, 129:131], T.q2[0:1, 0:2], AluOpType.subtract).then_inc(S.prdy, 1)
    V.wait_ge(S.pe3, 1)
    V.tensor_tensor(T.c_sb[:, :], T.a_sb[:, :], T.pq[:, 0:128], AluOpType.subtract).then_inc(S.crdy, 1)

    g.sync.wait_ge(S.crdy, 1)
    g.sync.dma_start(T.c[0:127, :], T.c_sb[1:128, :]).then_inc(S.stc, 16)
    g.scalar.wait_ge(S.mrdy, 1)
    g.scalar.dma_start(T.m[:, :], T.mext[0:1, 1:129]).then_inc(S.stm, 16)
    g.scalar.wait_ge(S.prdy, 1)
    g.scalar.dma_start(T.c[127:128, 126:128], T.crn[0:1, 0:2]).then_inc(S.stp, 16)
    g.scalar.wait_ge(S.crdy, 1)
    g.scalar.dma_start(T.c[127:128, 0:126], T.c_sb[1:127, 127:128]).then_inc(S.stk, 16)
    g.sync.wait_ge(S.stc, 16)
    g.scalar.wait_ge(S.stm, 16)
    g.scalar.wait_ge(S.stp, 16)
    g.scalar.wait_ge(S.stk, 16)
    g.wait_ge(S.ls, 16)


def rank_program(g, core, T, topo):
    cores = list(T.cores)
    chips = sorted(set(topo.chip(c) for c in cores))
    d_rows = 128 * len(cores)
    rank = T.rank_of(core)
    if rank is not None:
        mine = [c for c in cores if topo.chip(c) == topo.chip(core)]
        slot = mine.index(core)
        hs = [c + 2 for c in mine]
        order = [hs[0], hs[2], hs[1], hs[3]] if slot < 2 else [hs[2], hs[0], hs[3], hs[1]]
        _rank(g, core, T, topo, slot, order)
        return
    own = core - 2
    if own in cores:
        other = chips[1] if topo.chip(core) == chips[0] else chips[0]
        far = other * 8 + own % 8
        blocks = [0, 1, 2, 3] if own % 8 < 4 else [2, 3, 0, 1]
        _helper(g, core, T, topo, own, far, d_rows, blocks)
